import numpy as np
import ml_dtypes


def mxq(x, axis, fmt="e4m3"):
    dtype, down = {"e4m3": (ml_dtypes.float8_e4m3fn, 7), "e5m2": (ml_dtypes.float8_e5m2, 14)}[fmt]
    v = np.moveaxis(np.asarray(x, np.float32).astype(ml_dtypes.bfloat16).astype(np.float64), axis, -1)
    blocks = v.reshape(v.shape[:-1] + (-1, 32))
    amax = np.abs(blocks).max(-1, keepdims=True)
    byte = np.maximum(np.where(amax > 0, np.frexp(amax)[1] - 1 + 127, 0) - down, 1)
    scale = np.exp2(byte - 127.0)
    codes = (blocks / scale).astype(np.float32).astype(dtype).astype(np.float64)
    return np.moveaxis((codes * scale).reshape(v.shape), -1, axis)


WIDE = False


def mx_kscale(k):
    if not WIDE:
        return np.ones(k)
    levels = np.array([10, -10, 5, -5, 0])
    if k % 512:
        return np.exp2(np.random.permutation(np.resize(levels, k // 32))).repeat(32)
    a = np.empty((k // 512, 16))
    for p in range(k // 512):
        a[p, :8] = np.random.permutation(np.resize(levels, 8))
        for g in range(8):
            far = levels[np.abs(levels - a[p, g]) >= 10]
            a[p, g + 8] = far[np.random.randint(len(far))]
    return np.exp2(a.ravel()).repeat(32)


def f64(x):
    return np.asarray(x).astype(np.float64)


def striped(idx):
    return np.tile(np.asarray(idx).reshape(-1, 16).T, (8, 1)).astype(np.uint16)


def unstriped(offs):
    return offs[:16].T.reshape(-1).astype(np.int64)


E2M1 = np.array([0.0, 0.5, 1.0, 1.5, 2.0, 3.0, 4.0, 6.0, -0.0, -0.5, -1.0, -1.5, -2.0, -3.0, -4.0, -6.0])


def pack_weight(w, fmt):
    k, n = w.shape
    w = f64(np.asarray(w, np.float32).astype(ml_dtypes.bfloat16)).reshape(k // 32, 32, n)
    amax = np.abs(w).max(1)
    if fmt == "e4m3":
        byte = np.frexp(amax)[1] - 1 + 127 - 7
    else:
        mant, ex = np.frexp(amax / 6.0)
        byte = np.where(mant > 0.5, ex, ex - 1) + 127
    byte = np.clip(np.where(amax > 0, byte, 1), 1, 254)
    scaled = (w * np.exp2(127.0 - byte)[:, None, :]).reshape(k, n).astype(np.float32)
    by_word = np.ascontiguousarray(scaled.reshape(k // 512, 128, 4, n).transpose(0, 1, 3, 2))
    if fmt == "e4m3":
        words = by_word.astype(ml_dtypes.float8_e4m3fn).view(np.uint8)
    else:
        c = by_word.astype(ml_dtypes.float4_e2m1fn).view(np.uint8) & 0xF
        words = (c[..., 0::2] | (c[..., 1::2] << 4)).reshape(k // 512, 128, 2 * n)
    return np.ascontiguousarray(words), np.ascontiguousarray(byte.astype(np.uint8).reshape(k // 512, 16, n))


def unpack_weight(words, scales, fmt):
    g, _, n = scales.shape
    words = np.ascontiguousarray(words).reshape(g, 128, n, -1)
    if fmt == "e4m3":
        vals = words.view(ml_dtypes.float8_e4m3fn).astype(np.float64)
    else:
        nib = np.empty((g, 128, n, 4), np.uint8)
        nib[..., 0::2] = words & 0xF
        nib[..., 1::2] = words >> 4
        vals = E2M1[nib]
    vals = vals * np.repeat(np.exp2(scales.astype(np.float64) - 127.0), 8, axis=1)[..., None]
    return vals.transpose(0, 1, 3, 2).reshape(g * 512, n)


def sigmoid(v):
    return 1.0 / (1.0 + np.exp(-v))


K, R, F, T, J, M, N = 512, 128, 512, 2048, 512, 512, 64


def setup_inputs():
    n = np.random.standard_normal
    idx = np.random.permutation(T)[:J]
    idx2 = np.random.permutation(J)[:M]
    idx3 = np.random.permutation(M)[:N]
    fk = mx_kscale(K)
    ff = mx_kscale(F)
    tabp = pack_weight(n((K, T)) / fk[:, None], "e2m1")
    return {
        "tab_words": tabp[0],
        "tab_scales": tabp[1],
        "w1": (n((K, R)) * 1 / np.sqrt(K) * fk[:, None]).astype(np.float32),
        "gain": (np.random.uniform(0.5, 1.5, (R, 1))).astype(np.float32),
        "pb": (np.random.uniform(-0.5, 0.5, (1, M))).astype(np.float32),
        "mix": (np.random.uniform(0.7, 2.0, (R, 1))).astype(np.float32),
        "wo": (n((F, R)) * 1 / np.sqrt(F) * ff[:, None]).astype(np.float32),
        "dy": (n((F, N)) / ff[:, None]).astype(np.float32),
        "og": (np.random.uniform(0.3, 1.0, (R, 1))).astype(np.float32),
        "base": (0.3 * n((R, J))).astype(np.float32),
        "offs": striped(idx),
        "offs2": striped(idx2),
        "offs3": striped(idx3),
    }


def reference(tab_words, tab_scales, w1, gain, pb, mix, wo, dy, og, base, offs, offs2, offs3):
    idx = unstriped(offs)
    idx2 = unstriped(offs2)
    idx3 = unstriped(offs3)
    tabu = unpack_weight(tab_words, tab_scales, "e2m1")
    w1q = mxq(f64(w1), 0, "e4m3")
    tabidxg = tabu[:, idx]
    a = w1q.T @ tabidxg
    h1 = np.tanh(a)
    h2 = h1 * f64(gain)
    s = h2[:, idx2] + f64(pb)
    v1 = s[:, idx3] * f64(mix)
    woq = mxq(f64(wo), 0, "e4m3")
    dyq = mxq(f64(dy), 0, "e4m3")
    c0 = woq.T @ dyq
    dv1 = c0 * sigmoid(v1) * (1.0 + v1 * (1.0 - sigmoid(v1)))
    e1 = dv1 * f64(mix)
    s1 = np.zeros((R, M))
    s1[:, idx3] = e1
    s2 = np.zeros((R, J))
    s2[:, idx2] = s1
    dh1 = s2 * f64(gain)
    da = dh1 * (1.0 - np.square(h1))
    hda = da * 2.0
    hdh1 = hda * (1.0 - np.square(h1))
    hs2 = hdh1 * f64(gain)
    hs1 = hs2[:, idx2]
    he1 = hs1[:, idx3]
    hdv1 = he1 * f64(mix)
    hv1 = hdv1 * c0 * (1.0 + v1 * (1.0 - sigmoid(v1))) * sigmoid(v1) * (1.0 - sigmoid(v1)) + hdv1 * c0 * sigmoid(v1) * (1.0 - sigmoid(v1)) + hdv1 * c0 * sigmoid(v1) * v1 * (-1.0) * sigmoid(v1) * (1.0 - sigmoid(v1))
    e51 = hv1 * f64(mix)
    s51 = np.zeros((R, M))
    s51[:, idx3] = e51
    s52 = np.zeros((R, J))
    s52[:, idx2] = s51
    hh1 = hda * dh1 * (-1.0) * h1 * 2.0 + s52 * f64(gain)
    ha = hh1 * (1.0 - np.square(h1))
    y = ha * f64(og) + f64(base)
    return y

@@ -1,0 +1,201 @@
+from contextlib import ExitStack
+
+import concourse.mybir as mybir
+from concourse.masks import make_identity
+
+K, R, F, T, J, M, N = 512, 128, 512, 2048, 512, 512, 64
+FLOPS = 2 * K * R * J + 2 * F * R * N
+
+F32 = mybir.dt.float32
+BF16 = mybir.dt.bfloat16
+I32 = mybir.dt.int32
+U32 = mybir.dt.uint32
+U16 = mybir.dt.uint16
+U8 = mybir.dt.uint8
+FP8X4 = mybir.dt.float8_e4m3fn_x4
+FP4X4 = mybir.dt.float4_e2m1fn_x4
+ACT = mybir.ActivationFunctionType
+MULT, ADD, SUB = mybir.AluOpType.mult, mybir.AluOpType.add, mybir.AluOpType.subtract
+
+P = 128
+PACK = 4
+HALF = J // 2
+ADD_WINDOW = J + 8
+COPY_WINDOW = J + 192
+
+
+def interleave_views(grouped, raw):
+    return (
+        grouped[:].rearrange("p (c i) t -> p c t i", i=4),
+        raw[:].rearrange("p t (c i) -> p c t i", i=4),
+    )
+
+
+def tile_attend_gptwohops_kernel(tc, tab_words, tab_scales, w1, gain, pb, mix, wo, dy, og, base, offs, offs2, offs3, out):
+    nc = tc.nc
+    with ExitStack() as ctx:
+        lists = ctx.enter_context(tc.tile_pool(name="lists", bufs=1))
+        sb = ctx.enter_context(tc.tile_pool(name="sb", bufs=1))
+        ps = ctx.enter_context(tc.psum_pool(name="ps", bufs=1))
+
+        def f32(name, cols, tag=None):
+            return sb.tile([P, cols], F32, name=name, tag=tag or name, align_bytes=64)
+
+        idx = lists.tile([P, J // 16], U16, name="idx")
+        idx2 = lists.tile([P, M // 16], U16, name="idx2")
+        idx3 = lists.tile([P, N // 16], U16, name="idx3")
+
+        scales = sb.tile([P, T], U8, name="scales", align_bytes=64)
+        nc.vector.memset(scales[:].bitcast(I32), 0)
+        nc.sync.dma_start(idx[:], offs)
+        for quad in range(4):
+            nc.sync.dma_start(scales[32 * quad : 32 * quad + 4, :].bitcast(I32), tab_scales[0, 4 * quad : 4 * quad + 4, :].bitcast(I32))
+        w1_raw = sb.tile([P, PACK, R], F32, name="w1_raw", align_bytes=64)
+        nc.sync.dma_start(w1_raw[:], w1.rearrange("(p t) r -> p t r", t=PACK))
+        words = sb.tile([P, T], U16, name="words", align_bytes=64)
+        nc.sync.dma_start(words[:].bitcast(I32), tab_words[0].bitcast(I32))
+        pb_cols = f32("pb_cols", 4)
+        nc.gpsimd.dma_start(pb_cols[:], pb[0].rearrange("(p c) -> p c", c=4))
+        gain_c = f32("gain_c", 1)
+        nc.gpsimd.dma_start(gain_c[:], gain)
+        wo_raw = sb.tile([P, PACK, R], F32, name="wo_raw", align_bytes=64)
+        nc.sync.dma_start(wo_raw[:], wo.rearrange("(p t) r -> p t r", t=PACK))
+        dy_raw = sb.tile([P, PACK, N], F32, name="dy_raw", align_bytes=64)
+        nc.sync.dma_start(dy_raw[:], dy.rearrange("(p t) n -> p t n", t=PACK))
+        mix_c = f32("mix_c", 1)
+        nc.gpsimd.dma_start(mix_c[:], mix)
+        og_c = f32("og_c", 1)
+        nc.gpsimd.dma_start(og_c[:], og)
+        nc.sync.dma_start(idx2[:], offs2)
+        nc.sync.dma_start(idx3[:], offs3)
+        base_sb = f32("base_sb", J)
+        nc.sync.dma_start(base_sb[:], base)
+
+        h2 = f32("h2", ADD_WINDOW)
+        hs2 = f32("hs2", COPY_WINDOW)
+        s1 = f32("s1", M)
+        s51 = f32("s51", M)
+        nc.vector.memset(h2[:, J:], 0.0)
+        nc.vector.memset(hs2[:, J:], 0.0)
+        nc.vector.memset(s1[:], 0.0)
+        nc.vector.memset(s51[:], 0.0)
+        ident = f32("ident", P)
+        make_identity(nc, ident[:])
+
+        w1_bf = sb.tile([P, R, PACK], BF16, name="w1_bf", align_bytes=64)
+        nc.scalar.copy(*interleave_views(w1_bf, w1_raw))
+        tab_sc = sb.tile([P, J], U8, name="tab_sc", align_bytes=64)
+        nc.vector.tensor_copy(tab_sc[:], scales[:].indirect(idx[:]))
+        w1_q = sb.tile([P, R], U32, name="w1_q", align_bytes=64)
+        w1_sc = sb.tile([P, R], U8, name="w1_sc", align_bytes=64)
+        nc.vector.quantize_mx(w1_q[:].bitcast(FP8X4), w1_sc[:], w1_bf[:].rearrange("p r t -> p (r t)"))
+
+        pb_ps = ps.tile([P, 4, P], F32, name="pb_ps")
+        for c in range(4):
+            nc.tensor.transpose(pb_ps[:, c, :], pb_cols[:, c : c + 1].to_broadcast([P, P]), ident[:])
+        pb_rows = f32("pb_rows", M)
+        nc.scalar.copy(pb_rows[:].rearrange("i (p c) -> i p c", c=4), pb_ps[:].rearrange("i c p -> i p c"))
+
+        h1 = f32("h1", J)
+        for half in range(2):
+            cols = slice(half * HALF, (half + 1) * HALF)
+            tab_w = sb.tile([P, HALF], U16, name="tab_w%d" % half, align_bytes=64)
+            nc.vector.tensor_copy(tab_w[:], words[:].indirect(idx[:, half * HALF // 16 : (half + 1) * HALF // 16]))
+            a_ps = ps.tile([P, HALF], F32, name="a_ps%d" % half)
+            nc.tensor.matmul_mx(a_ps[:], lhsT=w1_q[:].bitcast(FP8X4), lhsT_scale=w1_sc[:], rhs=tab_w[:].bitcast(FP4X4), rhs_scale=tab_sc[:, cols], start=True, stop=True)
+            nc.scalar.activation(h1[:, cols], a_ps[:], ACT.Tanh)
+
+        def scaled(name, col, factor):
+            made = f32(name, 1)
+            nc.gpsimd.tensor_scalar(made[:], col[:], factor, 0.0, MULT, ADD)
+            return made
+
+        neg_gain = scaled("neg_gain", gain_c, -1.0)
+        mix_b = f32("mix_b", N)
+        nc.gpsimd.tensor_copy(mix_b[:], mix_c[:].to_broadcast([P, N]))
+        mix_4 = scaled("mix_4", mix_c, 0.25)
+        neg_mix_4 = scaled("neg_mix_4", mix_c, -0.25)
+        gog = scaled("gog", og_c, gain_c[:])
+        neg_gog = scaled("neg_gog", og_c, neg_gain[:])
+        neg_4og = scaled("neg_4og", og_c, -4.0)
+
+        wo_bf = sb.tile([P, R, PACK], BF16, name="wo_bf", align_bytes=64)
+        nc.vector.tensor_copy(*interleave_views(wo_bf, wo_raw))
+        dy_bf = sb.tile([P, N, PACK], BF16, name="dy_bf", tag="dy_bf_then_s", align_bytes=64)
+        nc.vector.tensor_copy(*interleave_views(dy_bf, dy_raw))
+        wo_q = sb.tile([P, R], U32, name="wo_q", align_bytes=64)
+        wo_sc = sb.tile([P, R], U8, name="wo_sc", align_bytes=64)
+        nc.vector.quantize_mx(wo_q[:].bitcast(FP8X4), wo_sc[:], wo_bf[:].rearrange("p r t -> p (r t)"))
+        dy_q = sb.tile([P, N], U32, name="dy_q", align_bytes=64)
+        dy_sc = sb.tile([P, N], U8, name="dy_sc", align_bytes=64)
+        nc.vector.quantize_mx(dy_q[:].bitcast(FP8X4), dy_sc[:], dy_bf[:].rearrange("p n t -> p (n t)"))
+        c0_ps = ps.tile([P, N], F32, name="c0_ps")
+        nc.tensor.matmul_mx(c0_ps[:], lhsT=wo_q[:].bitcast(FP8X4), lhsT_scale=wo_sc[:], rhs=dy_q[:].bitcast(FP8X4), rhs_scale=dy_sc[:], start=True, stop=True)
+
+        for half in range(2):
+            cols = slice(half * HALF, (half + 1) * HALF)
+            nc.vector.tensor_scalar(h2[:, cols], h1[:, cols], gain_c[:], None, MULT)
+
+        cm = f32("cm", N)
+        nc.scalar.activation(cm[:], c0_ps[:], ACT.Copy, scale=mix_c[:])
+        h1_sq = f32("h1_sq", J)
+        nc.scalar.activation(h1_sq[:], h1[:], ACT.Square)
+        gq_sq = f32("gq_sq", J)
+        nc.scalar.activation(gq_sq[:], h1_sq[:], ACT.Square, bias=gain_c[:], scale=neg_gain[:])
+
+        s = f32("s", M, tag="dy_bf_then_s")
+        nc.vector.tensor_tensor(s[:], h2[:].indirect(idx2[:]), pb_rows[:], ADD)
+        v1 = f32("v1", N, tag="v1_then_h1_out")
+        nc.vector.tensor_tensor(v1[:], s[:].indirect(idx3[:]), mix_b[:], MULT)
+        th = f32("th", N)
+        nc.scalar.activation(th[:], v1[:], ACT.Tanh, scale=0.5)
+        tm = f32("tm", N)
+        nc.scalar.activation(tm[:], th[:], ACT.Identity, bias=neg_mix_4[:], scale=mix_4[:])
+        u = f32("u", N)
+        nc.vector.scalar_tensor_tensor(u[:], th[:], 1.0, v1[:], SUB, MULT)
+        q = f32("q", N)
+        nc.vector.scalar_tensor_tensor(q[:], th[:], 1.0, cm[:], ADD, MULT)
+        vt = f32("vt", N)
+        nc.vector.tensor_tensor(vt[:], th[:], v1[:], MULT)
+        w = f32("w", N)
+        nc.vector.tensor_scalar(w[:], u[:], -0.25, 0.5, MULT, ADD)
+        k1 = f32("k1", N)
+        nc.vector.tensor_tensor(k1[:], tm[:], q[:], MULT)
+        nc.vector.tensor_tensor(s1[:].indirect(idx3[:]), q[:], w[:], MULT)
+        curv = f32("curv", N)
+        nc.vector.scalar_tensor_tensor(curv[:], vt[:], 2.0, k1[:], SUB, MULT)
+        s2 = f32("s2", COPY_WINDOW)
+        nc.vector.tensor_copy(s2[:].indirect(idx2[:]), s1[:])
+
+        h1_out = f32("h1_out", J, tag="v1_then_h1_out")
+        nc.scalar.activation(h1_out[:], h1[:], ACT.Copy, scale=neg_4og[:])
+        lin = f32("lin", J)
+        nc.scalar.activation(lin[:], h1_sq[:], ACT.Identity, bias=gog[:], scale=neg_gog[:])
+        quad_c = f32("quad_c", J)
+        nc.gpsimd.tensor_tensor(quad_c[:], gq_sq[:], h1_out[:], MULT)
+
+        nc.vector.scalar_tensor_tensor(hs2[:, :J], s2[:, :J], 2.0, gq_sq[:], MULT, MULT)
+        s2_sq = f32("s2_sq", J)
+        nc.scalar.activation(s2_sq[:], s2[:, :J], ACT.Square)
+        direct = f32("direct", J)
+        nc.gpsimd.tensor_tensor(direct[:], s2_sq[:], quad_c[:], MULT)
+
+        hs1 = f32("hs1", M)
+        nc.vector.tensor_copy(hs1[:], hs2[:].indirect(idx2[:]))
+        e51 = f32("e51", N, tag="e51_then_rest")
+        nc.vector.tensor_tensor(e51[:], hs1[:].indirect(idx3[:]), curv[:], MULT)
+        nc.vector.tensor_copy(s51[:].indirect(idx3[:]), e51[:])
+        s52 = f32("s52", COPY_WINDOW)
+        nc.vector.tensor_copy(s52[:].indirect(idx2[:]), s51[:])
+        rest = f32("rest", J, tag="e51_then_rest")
+        nc.gpsimd.tensor_tensor(rest[:], direct[:], base_sb[:], ADD)
+
+        back = [f32("back%d" % half, HALF) for half in range(2)]
+        for half in range(2):
+            cols = slice(half * HALF, (half + 1) * HALF)
+            nc.vector.tensor_tensor(back[half][:], s52[:, cols], lin[:, cols], MULT)
+        for half, queue in enumerate((nc.sync, nc.scalar)):
+            cols = slice(half * HALF, (half + 1) * HALF)
+            y = f32("y%d" % half, HALF)
+            nc.vector.tensor_tensor(y[:], back[half][:], rest[:, cols], ADD)
+            queue.dma_start(out[:, cols], y[:])

@@ -45,31 +45,33 @@ def tile_attend_gptwohops_kernel(tc, tab_words, tab_scales, w1, gain, pb, mix, w
         idx2 = lists.tile([P, M // 16], U16, name="idx2")
         idx3 = lists.tile([P, N // 16], U16, name="idx3")
 
-        scales = sb.tile([P, T], U8, name="scales", align_bytes=64)
+        scales = sb.tile([P, T], U8, name="scales", tag="scales_then_codes", align_bytes=64)
         nc.vector.memset(scales[:].bitcast(I32), 0)
-        nc.sync.dma_start(idx[:], offs)
-        for quad in range(4):
-            nc.sync.dma_start(scales[32 * quad : 32 * quad + 4, :].bitcast(I32), tab_scales[0, 4 * quad : 4 * quad + 4, :].bitcast(I32))
         w1_raw = sb.tile([P, PACK, R], F32, name="w1_raw", align_bytes=64)
         nc.sync.dma_start(w1_raw[:], w1.rearrange("(p t) r -> p t r", t=PACK))
+        nc.sync.dma_start(idx[:], offs)
+        pb_cols = sb.tile([P, 2, 2], F32, name="pb_cols", align_bytes=64)
+        nc.sync.dma_start(pb_cols[:], pb[0].rearrange("(h p c) -> p h c", h=2, c=2))
         words = sb.tile([P, T], U16, name="words", align_bytes=64)
         nc.sync.dma_start(words[:].bitcast(I32), tab_words[0].bitcast(I32))
-        pb_cols = f32("pb_cols", 4)
-        nc.gpsimd.dma_start(pb_cols[:], pb[0].rearrange("(p c) -> p c", c=4))
-        gain_c = f32("gain_c", 1)
-        nc.gpsimd.dma_start(gain_c[:], gain)
+        for quad in range(4):
+            nc.sync.dma_start(scales[32 * quad : 32 * quad + 4, :].bitcast(I32), tab_scales[0, 4 * quad : 4 * quad + 4, :].bitcast(I32))
         wo_raw = sb.tile([P, PACK, R], F32, name="wo_raw", align_bytes=64)
         nc.sync.dma_start(wo_raw[:], wo.rearrange("(p t) r -> p t r", t=PACK))
-        dy_raw = sb.tile([P, PACK, N], F32, name="dy_raw", align_bytes=64)
+        dy_raw = sb.tile([P, PACK, N], F32, name="dy_raw", tag="dy_raw_then_h1", align_bytes=64)
         nc.sync.dma_start(dy_raw[:], dy.rearrange("(p t) n -> p t n", t=PACK))
-        mix_c = f32("mix_c", 1)
-        nc.gpsimd.dma_start(mix_c[:], mix)
+        gain_c = f32("gain_c", 1)
+        nc.sync.dma_start(gain_c[:], gain)
         og_c = f32("og_c", 1)
-        nc.gpsimd.dma_start(og_c[:], og)
+        nc.sync.dma_start(og_c[:], og)
+        mix_c = f32("mix_c", 1)
+        nc.sync.dma_start(mix_c[:], mix)
         nc.sync.dma_start(idx2[:], offs2)
         nc.sync.dma_start(idx3[:], offs3)
         base_sb = f32("base_sb", J)
         nc.sync.dma_start(base_sb[:], base)
+        ident = f32("ident", P)
+        make_identity(nc, ident[:])
 
         h2 = f32("h2", ADD_WINDOW)
         hs2 = f32("hs2", COPY_WINDOW)
@@ -79,30 +81,34 @@ def tile_attend_gptwohops_kernel(tc, tab_words, tab_scales, w1, gain, pb, mix, w
         nc.vector.memset(hs2[:, J:], 0.0)
         nc.vector.memset(s1[:], 0.0)
         nc.vector.memset(s51[:], 0.0)
-        ident = f32("ident", P)
-        make_identity(nc, ident[:])
 
         w1_bf = sb.tile([P, R, PACK], BF16, name="w1_bf", align_bytes=64)
-        nc.scalar.copy(*interleave_views(w1_bf, w1_raw))
-        tab_sc = sb.tile([P, J], U8, name="tab_sc", align_bytes=64)
-        nc.vector.tensor_copy(tab_sc[:], scales[:].indirect(idx[:]))
+        nc.vector.tensor_copy(*interleave_views(w1_bf, w1_raw))
         w1_q = sb.tile([P, R], U32, name="w1_q", align_bytes=64)
         w1_sc = sb.tile([P, R], U8, name="w1_sc", align_bytes=64)
         nc.vector.quantize_mx(w1_q[:].bitcast(FP8X4), w1_sc[:], w1_bf[:].rearrange("p r t -> p (r t)"))
+        tab_w = sb.tile([P, J], U16, name="tab_w", align_bytes=64)
+        nc.vector.tensor_copy(tab_w[:], words[:].indirect(idx[:]))
 
-        pb_ps = ps.tile([P, 4, P], F32, name="pb_ps")
-        for c in range(4):
-            nc.tensor.transpose(pb_ps[:, c, :], pb_cols[:, c : c + 1].to_broadcast([P, P]), ident[:])
         pb_rows = f32("pb_rows", M)
-        nc.scalar.copy(pb_rows[:].rearrange("i (p c) -> i p c", c=4), pb_ps[:].rearrange("i c p -> i p c"))
+        for pair in range(2):
+            pb_ps = ps.tile([P, 2, P], F32, name="pb_ps%d" % pair, tag="bank%d" % pair)
+            for c in range(2):
+                nc.tensor.transpose(pb_ps[:, c, :], pb_cols[:, pair, c : c + 1].to_broadcast([P, P]), ident[:])
+            nc.scalar.copy(pb_rows[:, pair * HALF : (pair + 1) * HALF].rearrange("i (p c) -> i p c", c=2), pb_ps[:].rearrange("i c p -> i p c"))
 
-        h1 = f32("h1", J)
+        wo_bf = sb.tile([P, R, PACK], BF16, name="wo_bf", align_bytes=64)
+        nc.scalar.copy(*interleave_views(wo_bf, wo_raw))
+        dy_bf = sb.tile([P, N, PACK], BF16, name="dy_bf", tag="dy_bf_then_s", align_bytes=64)
+        nc.scalar.copy(*interleave_views(dy_bf, dy_raw))
+
+        h1 = f32("h1", J, tag="dy_raw_then_h1")
         for half in range(2):
             cols = slice(half * HALF, (half + 1) * HALF)
-            tab_w = sb.tile([P, HALF], U16, name="tab_w%d" % half, align_bytes=64)
-            nc.vector.tensor_copy(tab_w[:], words[:].indirect(idx[:, half * HALF // 16 : (half + 1) * HALF // 16]))
-            a_ps = ps.tile([P, HALF], F32, name="a_ps%d" % half)
-            nc.tensor.matmul_mx(a_ps[:], lhsT=w1_q[:].bitcast(FP8X4), lhsT_scale=w1_sc[:], rhs=tab_w[:].bitcast(FP4X4), rhs_scale=tab_sc[:, cols], start=True, stop=True)
+            tab_sc = sb.tile([P, HALF], U8, name="tab_sc%d" % half, align_bytes=64)
+            nc.vector.tensor_copy(tab_sc[:], scales[:].indirect(idx[:, half * HALF // 16 : (half + 1) * HALF // 16]))
+            a_ps = ps.tile([P, HALF], F32, name="a_ps%d" % half, tag="bank%d" % half)
+            nc.tensor.matmul_mx(a_ps[:], lhsT=w1_q[:].bitcast(FP8X4), lhsT_scale=w1_sc[:], rhs=tab_w[:, cols].bitcast(FP4X4), rhs_scale=tab_sc[:], start=True, stop=True)
             nc.scalar.activation(h1[:, cols], a_ps[:], ACT.Tanh)
 
         def scaled(name, col, factor):
@@ -114,88 +120,83 @@ def tile_attend_gptwohops_kernel(tc, tab_words, tab_scales, w1, gain, pb, mix, w
         mix_b = f32("mix_b", N)
         nc.gpsimd.tensor_copy(mix_b[:], mix_c[:].to_broadcast([P, N]))
         mix_4 = scaled("mix_4", mix_c, 0.25)
-        neg_mix_4 = scaled("neg_mix_4", mix_c, -0.25)
+        mix_2 = scaled("mix_2", mix_c, 0.5)
         gog = scaled("gog", og_c, gain_c[:])
         neg_gog = scaled("neg_gog", og_c, neg_gain[:])
         neg_4og = scaled("neg_4og", og_c, -4.0)
 
-        wo_bf = sb.tile([P, R, PACK], BF16, name="wo_bf", align_bytes=64)
-        nc.vector.tensor_copy(*interleave_views(wo_bf, wo_raw))
-        dy_bf = sb.tile([P, N, PACK], BF16, name="dy_bf", tag="dy_bf_then_s", align_bytes=64)
-        nc.vector.tensor_copy(*interleave_views(dy_bf, dy_raw))
-        wo_q = sb.tile([P, R], U32, name="wo_q", align_bytes=64)
+        codes = sb.tile([P, R + N], U32, name="codes", tag="scales_then_codes", align_bytes=64)
+        wo_q, dy_q = codes[:, :R], codes[:, R:]
         wo_sc = sb.tile([P, R], U8, name="wo_sc", align_bytes=64)
-        nc.vector.quantize_mx(wo_q[:].bitcast(FP8X4), wo_sc[:], wo_bf[:].rearrange("p r t -> p (r t)"))
-        dy_q = sb.tile([P, N], U32, name="dy_q", align_bytes=64)
+        nc.vector.quantize_mx(wo_q.bitcast(FP8X4), wo_sc[:], wo_bf[:].rearrange("p r t -> p (r t)"))
         dy_sc = sb.tile([P, N], U8, name="dy_sc", align_bytes=64)
-        nc.vector.quantize_mx(dy_q[:].bitcast(FP8X4), dy_sc[:], dy_bf[:].rearrange("p n t -> p (n t)"))
-        c0_ps = ps.tile([P, N], F32, name="c0_ps")
-        nc.tensor.matmul_mx(c0_ps[:], lhsT=wo_q[:].bitcast(FP8X4), lhsT_scale=wo_sc[:], rhs=dy_q[:].bitcast(FP8X4), rhs_scale=dy_sc[:], start=True, stop=True)
+        nc.vector.quantize_mx(dy_q.bitcast(FP8X4), dy_sc[:], dy_bf[:].rearrange("p n t -> p (n t)"))
+        c0_ps = ps.tile([P, N], F32, name="c0_ps", tag="bank0")
+        nc.tensor.matmul_mx(c0_ps[:], lhsT=wo_q.bitcast(FP8X4), lhsT_scale=wo_sc[:], rhs=dy_q.bitcast(FP8X4), rhs_scale=dy_sc[:], start=True, stop=True)
 
         for half in range(2):
             cols = slice(half * HALF, (half + 1) * HALF)
             nc.vector.tensor_scalar(h2[:, cols], h1[:, cols], gain_c[:], None, MULT)
 
+        halves = [slice(0, HALF), slice(HALF, J)]
         cm = f32("cm", N)
         nc.scalar.activation(cm[:], c0_ps[:], ACT.Copy, scale=mix_c[:])
-        h1_sq = f32("h1_sq", J)
+        h1_sq = f32("h1_sq", J, tag="h1_sq_then_th")
         nc.scalar.activation(h1_sq[:], h1[:], ACT.Square)
         gq_sq = f32("gq_sq", J)
         nc.scalar.activation(gq_sq[:], h1_sq[:], ACT.Square, bias=gain_c[:], scale=neg_gain[:])
+        lin = f32("lin", J)
+        nc.scalar.activation(lin[:], h1_sq[:], ACT.Identity, bias=gog[:], scale=neg_gog[:])
 
         s = f32("s", M, tag="dy_bf_then_s")
         nc.vector.tensor_tensor(s[:], h2[:].indirect(idx2[:]), pb_rows[:], ADD)
-        v1 = f32("v1", N, tag="v1_then_h1_out")
+        v1 = f32("v1", N)
         nc.vector.tensor_tensor(v1[:], s[:].indirect(idx3[:]), mix_b[:], MULT)
-        th = f32("th", N)
+        th = f32("th", N, tag="h1_sq_then_th")
         nc.scalar.activation(th[:], v1[:], ACT.Tanh, scale=0.5)
-        tm = f32("tm", N)
-        nc.scalar.activation(tm[:], th[:], ACT.Identity, bias=neg_mix_4[:], scale=mix_4[:])
         u = f32("u", N)
         nc.vector.scalar_tensor_tensor(u[:], th[:], 1.0, v1[:], SUB, MULT)
         q = f32("q", N)
         nc.vector.scalar_tensor_tensor(q[:], th[:], 1.0, cm[:], ADD, MULT)
-        vt = f32("vt", N)
-        nc.vector.tensor_tensor(vt[:], th[:], v1[:], MULT)
         w = f32("w", N)
         nc.vector.tensor_scalar(w[:], u[:], -0.25, 0.5, MULT, ADD)
-        k1 = f32("k1", N)
-        nc.vector.tensor_tensor(k1[:], tm[:], q[:], MULT)
         nc.vector.tensor_tensor(s1[:].indirect(idx3[:]), q[:], w[:], MULT)
-        curv = f32("curv", N)
-        nc.vector.scalar_tensor_tensor(curv[:], vt[:], 2.0, k1[:], SUB, MULT)
         s2 = f32("s2", COPY_WINDOW)
         nc.vector.tensor_copy(s2[:].indirect(idx2[:]), s1[:])
-
-        h1_out = f32("h1_out", J, tag="v1_then_h1_out")
-        nc.scalar.activation(h1_out[:], h1[:], ACT.Copy, scale=neg_4og[:])
-        lin = f32("lin", J)
-        nc.scalar.activation(lin[:], h1_sq[:], ACT.Identity, bias=gog[:], scale=neg_gog[:])
-        quad_c = f32("quad_c", J)
-        nc.gpsimd.tensor_tensor(quad_c[:], gq_sq[:], h1_out[:], MULT)
-
         nc.vector.scalar_tensor_tensor(hs2[:, :J], s2[:, :J], 2.0, gq_sq[:], MULT, MULT)
-        s2_sq = f32("s2_sq", J)
-        nc.scalar.activation(s2_sq[:], s2[:, :J], ACT.Square)
-        direct = f32("direct", J)
-        nc.gpsimd.tensor_tensor(direct[:], s2_sq[:], quad_c[:], MULT)
-
         hs1 = f32("hs1", M)
         nc.vector.tensor_copy(hs1[:], hs2[:].indirect(idx2[:]))
-        e51 = f32("e51", N, tag="e51_then_rest")
+
+        vt = f32("vt", N)
+        nc.vector.scalar_tensor_tensor(vt[:], v1[:], mix_4[:], th[:], MULT, MULT)
+        k1 = f32("k1", N)
+        nc.vector.scalar_tensor_tensor(k1[:], th[:], 1.0, q[:], SUB, MULT)
+        curv = f32("curv", N)
+        nc.vector.scalar_tensor_tensor(curv[:], vt[:], mix_2[:], k1[:], SUB, MULT)
+
+        e51 = f32("e51", N)
         nc.vector.tensor_tensor(e51[:], hs1[:].indirect(idx3[:]), curv[:], MULT)
         nc.vector.tensor_copy(s51[:].indirect(idx3[:]), e51[:])
         s52 = f32("s52", COPY_WINDOW)
         nc.vector.tensor_copy(s52[:].indirect(idx2[:]), s51[:])
-        rest = f32("rest", J, tag="e51_then_rest")
-        nc.gpsimd.tensor_tensor(rest[:], direct[:], base_sb[:], ADD)
 
-        back = [f32("back%d" % half, HALF) for half in range(2)]
-        for half in range(2):
-            cols = slice(half * HALF, (half + 1) * HALF)
-            nc.vector.tensor_tensor(back[half][:], s52[:, cols], lin[:, cols], MULT)
-        for half, queue in enumerate((nc.sync, nc.scalar)):
-            cols = slice(half * HALF, (half + 1) * HALF)
-            y = f32("y%d" % half, HALF)
-            nc.vector.tensor_tensor(y[:], back[half][:], rest[:, cols], ADD)
-            queue.dma_start(out[:, cols], y[:])
+        quad_c = f32("quad_c", J)
+        s2_sq = f32("s2_sq", J)
+        direct = f32("direct", J)
+        rest = f32("rest", J)
+        for cols in halves:
+            nc.vector.scalar_tensor_tensor(quad_c[:, cols], gq_sq[:, cols], neg_4og[:], h1[:, cols], MULT, MULT)
+        for cols in halves:
+            nc.scalar.activation(s2_sq[:, cols], s2[:, cols], ACT.Square)
+        for cols in halves:
+            nc.vector.tensor_tensor(direct[:, cols], s2_sq[:, cols], quad_c[:, cols], MULT)
+        for cols in halves:
+            nc.vector.tensor_tensor(rest[:, cols], direct[:, cols], base_sb[:, cols], ADD)
+
+        back = f32("back", J)
+        for cols in halves:
+            nc.vector.tensor_tensor(back[:, cols], s52[:, cols], lin[:, cols], MULT)
+        y = f32("y", J)
+        for cols, queue in zip(halves, (nc.sync, nc.scalar)):
+            nc.vector.tensor_tensor(y[:, cols], back[:, cols], rest[:, cols], ADD)
+            queue.dma_start(out[:, cols], y[:, cols])

from contextlib import ExitStack

import concourse.mybir as mybir
from concourse.masks import make_identity

K, R, F, T, J, M, N = 512, 128, 512, 2048, 512, 512, 64
FLOPS = 2 * K * R * J + 2 * F * R * N

F32 = mybir.dt.float32
BF16 = mybir.dt.bfloat16
I32 = mybir.dt.int32
U32 = mybir.dt.uint32
U16 = mybir.dt.uint16
U8 = mybir.dt.uint8
FP8X4 = mybir.dt.float8_e4m3fn_x4
FP4X4 = mybir.dt.float4_e2m1fn_x4
ACT = mybir.ActivationFunctionType
MULT, ADD, SUB = mybir.AluOpType.mult, mybir.AluOpType.add, mybir.AluOpType.subtract

P = 128
PACK = 4
HALF = J // 2
ADD_WINDOW = J + 8
COPY_WINDOW = J + 192


def interleave_views(grouped, raw):
    return (
        grouped[:].rearrange("p (c i) t -> p c t i", i=4),
        raw[:].rearrange("p t (c i) -> p c t i", i=4),
    )


def tile_attend_gptwohops_kernel(tc, tab_words, tab_scales, w1, gain, pb, mix, wo, dy, og, base, offs, offs2, offs3, out):
    nc = tc.nc
    with ExitStack() as ctx:
        lists = ctx.enter_context(tc.tile_pool(name="lists", bufs=1))
        sb = ctx.enter_context(tc.tile_pool(name="sb", bufs=1))
        ps = ctx.enter_context(tc.psum_pool(name="ps", bufs=1))

        def f32(name, cols, tag=None):
            return sb.tile([P, cols], F32, name=name, tag=tag or name, align_bytes=64)

        idx = lists.tile([P, J // 16], U16, name="idx")
        idx2 = lists.tile([P, M // 16], U16, name="idx2")
        idx3 = lists.tile([P, N // 16], U16, name="idx3")

        scales = sb.tile([P, T], U8, name="scales", tag="scales_then_codes", align_bytes=64)
        nc.vector.memset(scales[:].bitcast(I32), 0)
        w1_raw = sb.tile([P, PACK, R], F32, name="w1_raw", align_bytes=64)
        nc.sync.dma_start(w1_raw[:], w1.rearrange("(p t) r -> p t r", t=PACK))
        nc.sync.dma_start(idx[:], offs)
        pb_cols = sb.tile([P, 2, 2], F32, name="pb_cols", align_bytes=64)
        nc.sync.dma_start(pb_cols[:], pb[0].rearrange("(h p c) -> p h c", h=2, c=2))
        words = sb.tile([P, T], U16, name="words", align_bytes=64)
        nc.sync.dma_start(words[:].bitcast(I32), tab_words[0].bitcast(I32))
        for quad in range(4):
            nc.sync.dma_start(scales[32 * quad : 32 * quad + 4, :].bitcast(I32), tab_scales[0, 4 * quad : 4 * quad + 4, :].bitcast(I32))
        wo_raw = sb.tile([P, PACK, R], F32, name="wo_raw", align_bytes=64)
        nc.sync.dma_start(wo_raw[:], wo.rearrange("(p t) r -> p t r", t=PACK))
        dy_raw = sb.tile([P, PACK, N], F32, name="dy_raw", tag="dy_raw_then_h1", align_bytes=64)
        nc.sync.dma_start(dy_raw[:], dy.rearrange("(p t) n -> p t n", t=PACK))
        gain_c = f32("gain_c", 1)
        nc.sync.dma_start(gain_c[:], gain)
        og_c = f32("og_c", 1)
        nc.sync.dma_start(og_c[:], og)
        mix_c = f32("mix_c", 1)
        nc.sync.dma_start(mix_c[:], mix)
        nc.sync.dma_start(idx2[:], offs2)
        nc.sync.dma_start(idx3[:], offs3)
        base_sb = f32("base_sb", J)
        nc.sync.dma_start(base_sb[:], base)
        ident = f32("ident", P)
        make_identity(nc, ident[:])

        h2 = f32("h2", ADD_WINDOW)
        hs2 = f32("hs2", COPY_WINDOW)
        s1 = f32("s1", M)
        s51 = f32("s51", M)
        nc.vector.memset(h2[:, J:], 0.0)
        nc.vector.memset(hs2[:, J:], 0.0)
        nc.vector.memset(s1[:], 0.0)
        nc.vector.memset(s51[:], 0.0)

        w1_bf = sb.tile([P, R, PACK], BF16, name="w1_bf", align_bytes=64)
        nc.vector.tensor_copy(*interleave_views(w1_bf, w1_raw))
        w1_q = sb.tile([P, R], U32, name="w1_q", align_bytes=64)
        w1_sc = sb.tile([P, R], U8, name="w1_sc", align_bytes=64)
        nc.vector.quantize_mx(w1_q[:].bitcast(FP8X4), w1_sc[:], w1_bf[:].rearrange("p r t -> p (r t)"))
        tab_w = sb.tile([P, J], U16, name="tab_w", align_bytes=64)
        nc.vector.tensor_copy(tab_w[:], words[:].indirect(idx[:]))

        pb_rows = f32("pb_rows", M)
        for pair in range(2):
            pb_ps = ps.tile([P, 2, P], F32, name="pb_ps%d" % pair, tag="bank%d" % pair)
            for c in range(2):
                nc.tensor.transpose(pb_ps[:, c, :], pb_cols[:, pair, c : c + 1].to_broadcast([P, P]), ident[:])
            nc.scalar.copy(pb_rows[:, pair * HALF : (pair + 1) * HALF].rearrange("i (p c) -> i p c", c=2), pb_ps[:].rearrange("i c p -> i p c"))

        wo_bf = sb.tile([P, R, PACK], BF16, name="wo_bf", align_bytes=64)
        nc.scalar.copy(*interleave_views(wo_bf, wo_raw))
        dy_bf = sb.tile([P, N, PACK], BF16, name="dy_bf", tag="dy_bf_then_s", align_bytes=64)
        nc.scalar.copy(*interleave_views(dy_bf, dy_raw))

        h1 = f32("h1", J, tag="dy_raw_then_h1")
        for half in range(2):
            cols = slice(half * HALF, (half + 1) * HALF)
            tab_sc = sb.tile([P, HALF], U8, name="tab_sc%d" % half, align_bytes=64)
            nc.vector.tensor_copy(tab_sc[:], scales[:].indirect(idx[:, half * HALF // 16 : (half + 1) * HALF // 16]))
            a_ps = ps.tile([P, HALF], F32, name="a_ps%d" % half, tag="bank%d" % half)
            nc.tensor.matmul_mx(a_ps[:], lhsT=w1_q[:].bitcast(FP8X4), lhsT_scale=w1_sc[:], rhs=tab_w[:, cols].bitcast(FP4X4), rhs_scale=tab_sc[:], start=True, stop=True)
            nc.scalar.activation(h1[:, cols], a_ps[:], ACT.Tanh)

        def scaled(name, col, factor):
            made = f32(name, 1)
            nc.gpsimd.tensor_scalar(made[:], col[:], factor, 0.0, MULT, ADD)
            return made

        neg_gain = scaled("neg_gain", gain_c, -1.0)
        mix_b = f32("mix_b", N)
        nc.gpsimd.tensor_copy(mix_b[:], mix_c[:].to_broadcast([P, N]))
        mix_4 = scaled("mix_4", mix_c, 0.25)
        mix_2 = scaled("mix_2", mix_c, 0.5)
        gog = scaled("gog", og_c, gain_c[:])
        neg_gog = scaled("neg_gog", og_c, neg_gain[:])
        neg_4og = scaled("neg_4og", og_c, -4.0)

        codes = sb.tile([P, R + N], U32, name="codes", tag="scales_then_codes", align_bytes=64)
        wo_q, dy_q = codes[:, :R], codes[:, R:]
        wo_sc = sb.tile([P, R], U8, name="wo_sc", align_bytes=64)
        nc.vector.quantize_mx(wo_q.bitcast(FP8X4), wo_sc[:], wo_bf[:].rearrange("p r t -> p (r t)"))
        dy_sc = sb.tile([P, N], U8, name="dy_sc", align_bytes=64)
        nc.vector.quantize_mx(dy_q.bitcast(FP8X4), dy_sc[:], dy_bf[:].rearrange("p n t -> p (n t)"))
        c0_ps = ps.tile([P, N], F32, name="c0_ps", tag="bank0")
        nc.tensor.matmul_mx(c0_ps[:], lhsT=wo_q.bitcast(FP8X4), lhsT_scale=wo_sc[:], rhs=dy_q.bitcast(FP8X4), rhs_scale=dy_sc[:], start=True, stop=True)

        for half in range(2):
            cols = slice(half * HALF, (half + 1) * HALF)
            nc.vector.tensor_scalar(h2[:, cols], h1[:, cols], gain_c[:], None, MULT)

        halves = [slice(0, HALF), slice(HALF, J)]
        cm = f32("cm", N)
        nc.scalar.activation(cm[:], c0_ps[:], ACT.Copy, scale=mix_c[:])
        h1_sq = f32("h1_sq", J, tag="h1_sq_then_th")
        nc.scalar.activation(h1_sq[:], h1[:], ACT.Square)
        gq_sq = f32("gq_sq", J)
        nc.scalar.activation(gq_sq[:], h1_sq[:], ACT.Square, bias=gain_c[:], scale=neg_gain[:])
        lin = f32("lin", J)
        nc.scalar.activation(lin[:], h1_sq[:], ACT.Identity, bias=gog[:], scale=neg_gog[:])

        s = f32("s", M, tag="dy_bf_then_s")
        nc.vector.tensor_tensor(s[:], h2[:].indirect(idx2[:]), pb_rows[:], ADD)
        v1 = f32("v1", N)
        nc.vector.tensor_tensor(v1[:], s[:].indirect(idx3[:]), mix_b[:], MULT)
        th = f32("th", N, tag="h1_sq_then_th")
        nc.scalar.activation(th[:], v1[:], ACT.Tanh, scale=0.5)
        u = f32("u", N)
        nc.vector.scalar_tensor_tensor(u[:], th[:], 1.0, v1[:], SUB, MULT)
        q = f32("q", N)
        nc.vector.scalar_tensor_tensor(q[:], th[:], 1.0, cm[:], ADD, MULT)
        w = f32("w", N)
        nc.vector.tensor_scalar(w[:], u[:], -0.25, 0.5, MULT, ADD)
        nc.vector.tensor_tensor(s1[:].indirect(idx3[:]), q[:], w[:], MULT)
        s2 = f32("s2", COPY_WINDOW)
        nc.vector.tensor_copy(s2[:].indirect(idx2[:]), s1[:])
        nc.vector.scalar_tensor_tensor(hs2[:, :J], s2[:, :J], 2.0, gq_sq[:], MULT, MULT)
        hs1 = f32("hs1", M)
        nc.vector.tensor_copy(hs1[:], hs2[:].indirect(idx2[:]))

        vt = f32("vt", N)
        nc.vector.scalar_tensor_tensor(vt[:], v1[:], mix_4[:], th[:], MULT, MULT)
        k1 = f32("k1", N)
        nc.vector.scalar_tensor_tensor(k1[:], th[:], 1.0, q[:], SUB, MULT)
        curv = f32("curv", N)
        nc.vector.scalar_tensor_tensor(curv[:], vt[:], mix_2[:], k1[:], SUB, MULT)

        e51 = f32("e51", N)
        nc.vector.tensor_tensor(e51[:], hs1[:].indirect(idx3[:]), curv[:], MULT)
        nc.vector.tensor_copy(s51[:].indirect(idx3[:]), e51[:])
        s52 = f32("s52", COPY_WINDOW)
        nc.vector.tensor_copy(s52[:].indirect(idx2[:]), s51[:])

        quad_c = f32("quad_c", J)
        s2_sq = f32("s2_sq", J)
        direct = f32("direct", J)
        rest = f32("rest", J)
        for cols in halves:
            nc.vector.scalar_tensor_tensor(quad_c[:, cols], gq_sq[:, cols], neg_4og[:], h1[:, cols], MULT, MULT)
        for cols in halves:
            nc.scalar.activation(s2_sq[:, cols], s2[:, cols], ACT.Square)
        for cols in halves:
            nc.vector.tensor_tensor(direct[:, cols], s2_sq[:, cols], quad_c[:, cols], MULT)
        for cols in halves:
            nc.vector.tensor_tensor(rest[:, cols], direct[:, cols], base_sb[:, cols], ADD)

        back = f32("back", J)
        for cols in halves:
            nc.vector.tensor_tensor(back[:, cols], s52[:, cols], lin[:, cols], MULT)
        y = f32("y", J)
        for cols, queue in zip(halves, (nc.sync, nc.scalar)):
            nc.vector.tensor_tensor(y[:, cols], back[:, cols], rest[:, cols], ADD)
            queue.dma_start(out[:, cols], y[:, cols])
